import numpy as np
import ml_dtypes


def mxq(x, axis, fmt="e4m3"):
    dtype, down = {"e4m3": (ml_dtypes.float8_e4m3fn, 7), "e5m2": (ml_dtypes.float8_e5m2, 14)}[fmt]
    v = np.moveaxis(np.asarray(x, np.float32).astype(ml_dtypes.bfloat16).astype(np.float64), axis, -1)
    blocks = v.reshape(v.shape[:-1] + (-1, 32))
    amax = np.abs(blocks).max(-1, keepdims=True)
    byte = np.maximum(np.where(amax > 0, np.frexp(amax)[1] - 1 + 127, 0) - down, 1)
    scale = np.exp2(byte - 127.0)
    codes = (blocks / scale).astype(np.float32).astype(dtype).astype(np.float64)
    return np.moveaxis((codes * scale).reshape(v.shape), -1, axis)


WIDE = False


def mx_kscale(k):
    if not WIDE:
        return np.ones(k)
    levels = np.array([10, -10, 5, -5, 0])
    if k % 512:
        return np.exp2(np.random.permutation(np.resize(levels, k // 32))).repeat(32)
    a = np.empty((k // 512, 16))
    for p in range(k // 512):
        a[p, :8] = np.random.permutation(np.resize(levels, 8))
        for g in range(8):
            far = levels[np.abs(levels - a[p, g]) >= 10]
            a[p, g + 8] = far[np.random.randint(len(far))]
    return np.exp2(a.ravel()).repeat(32)


BF16 = ml_dtypes.bfloat16


def bf(x):
    return np.asarray(x, np.float32).astype(BF16)


def f64(x):
    return np.asarray(x).astype(np.float64)


B, N, D, K = 8, 512, 512, 256
EPS = 1e-5


def layer_norm_last(f, gain, bias):
    mu = np.mean(f, axis=-1, keepdims=True)
    centered = f - mu
    var = np.mean(centered * centered, axis=-1, keepdims=True)
    return centered / np.sqrt(var + EPS) * gain + bias


def draw0():
    s, u = mx_kscale(N), mx_kscale(D)
    x = 0.1 * np.random.standard_normal((B, N, D))
    e = 1.0 + 0.2 * np.random.standard_normal(N)
    y = (np.random.standard_normal((N, K)) + 0.5 * np.random.standard_normal((N, 1))) * 0.5 / np.sqrt(N)
    g = 1.0 + 0.2 * np.random.standard_normal(D)
    ln_g = 1.0 + 0.1 * np.random.standard_normal(K)
    ln_b = 0.3 * np.random.standard_normal(K)
    return {"x": bf(x * u), "e": bf(e * s), "y": bf(y / s[:, None]), "g": bf(g / (u * u)), "ln_g": bf(ln_g), "ln_b": bf(ln_b)}


def core(x, e, y, g, ln_g, ln_b):
    x, e, y, g, ln_g, ln_b = f64(x), f64(e), f64(y), f64(g), f64(ln_g), f64(ln_b)
    d = x.shape[-1]
    xe = x * e[None, :, None]
    m = np.swapaxes(mxq(xe, 1, "e4m3"), 1, 2) @ mxq(y, 0, "e4m3")
    mg = g[None, :, None] * m
    f = (mxq(x, 2, "e4m3") @ mxq(mg, 1, "e4m3")) / np.sqrt(d)
    return layer_norm_last(f, ln_g, ln_b)


def e4m3fn_bytes(y):
    return np.clip(np.asarray(y, np.float64), -448.0, 448.0).astype(np.float32).astype(ml_dtypes.float8_e4m3fn).view(np.uint8)


def e4m3fn_values(b):
    return np.asarray(b, np.uint8).view(ml_dtypes.float8_e4m3fn).astype(np.float64)


def setup_inputs():
    d = draw0()
    x0 = np.asarray(d['y']).astype(np.float64)
    s = (np.max(np.abs(x0), axis=(1,), keepdims=True) / 448.0).astype(np.float32)
    out = {}
    for k, v in d.items():
        if k == 'y':
            out['y_bytes'] = e4m3fn_bytes(x0 / s.astype(np.float64))
            out['y_scale'] = s
        else:
            out[k] = v
    return out


def reference(x, e, y_bytes, y_scale, g, ln_g, ln_b):
    return core(x, e, e4m3fn_values(y_bytes) * y_scale.astype(np.float64), g, ln_g, ln_b)

@@ -1,0 +1,268 @@
+from contextlib import ExitStack
+
+import concourse.mybir as mybir
+from concourse.masks import make_identity
+
+B, N, D, K = 8, 512, 512, 256
+EPS = 1e-5
+FLOPS = 2 * 2 * B * N * D * K
+
+F32 = mybir.dt.float32
+BF16 = mybir.dt.bfloat16
+U32 = mybir.dt.uint32
+U8 = mybir.dt.uint8
+FP8 = mybir.dt.float8_e4m3fn
+FP8X4 = mybir.dt.float8_e4m3fn_x4
+ACT = mybir.ActivationFunctionType
+ALU = mybir.AluOpType
+
+P = 128
+PACK = 4
+HALVES = 2
+TURN_BANKS = 3
+
+
+def tile_wukongfieldgainedlowrankfm_kernel(tc, x, e, y_bytes, y_scale, g, ln_g, ln_b, out):
+    nc = tc.nc
+    with ExitStack() as ctx:
+        keep = ctx.enter_context(tc.tile_pool(name="keep", bufs=1))
+        work = ctx.enter_context(tc.tile_pool(name="work", bufs=2))
+        psum = ctx.enter_context(tc.psum_pool(name="psum", bufs=1))
+        ctx.enter_context(tc.manual_schedule())
+
+        x_sb = {}
+
+        def load_x(b, h):
+            x_sb[b, h] = keep.tile([P, 2, D], BF16, name="x_%d_%d" % (b, h), align_bytes=256)
+            rows = x[b].rearrange("(p j) d -> p j d", j=PACK)
+            nc.sync.dma_start(out=x_sb[b, h][:], in_=rows[:, 2 * h : 2 * h + 2, :])
+
+        y_raw = keep.tile([P, PACK, K], U8, name="y_raw", align_bytes=256)
+        y_row_scale = keep.tile([P, PACK], F32, name="y_row_scale")
+        e_bf = keep.tile([P, PACK], BF16, name="e_bf")
+        g_bf = keep.tile([P, PACK], BF16, name="g_bf")
+        ln_g_bf = keep.tile([P, 2], BF16, name="ln_g_bf")
+        ln_b_bf = keep.tile([P, 2], BF16, name="ln_b_bf")
+
+        load_x(0, 0)
+        nc.sync.dma_start(out=y_raw[:], in_=y_bytes.rearrange("(p j) k -> p j k", j=PACK))
+        nc.scalar.dma_start(out=y_row_scale[:], in_=y_scale.rearrange("(p j) o -> p (j o)", j=PACK))
+        nc.scalar.dma_start(out=e_bf[:], in_=e.rearrange("(p j) -> p j", j=PACK))
+        load_x(0, 1)
+        nc.scalar.dma_start(out=g_bf[:], in_=g.rearrange("(p t) -> p t", t=PACK))
+        load_x(1, 0)
+        load_x(1, 1)
+        nc.sync.dma_start(out=ln_g_bf[:], in_=ln_g.rearrange("(p c) -> p c", c=2))
+        nc.sync.dma_start(out=ln_b_bf[:], in_=ln_b.rearrange("(p c) -> p c", c=2))
+        for b in range(2, B):
+            for h in range(HALVES):
+                load_x(b, h)
+
+        ident = keep.tile([P, P], F32, name="ident")
+        make_identity(nc, ident[:])
+
+        planes, xe_grouped, xe_q, xt_grouped, xt_q, mg_grouped, mg_q = {}, {}, {}, {}, {}, {}, {}
+        turn_bank, m_bank, f_bank, f_scaled, neg_mean, sq_sum, rstd, centred = {}, {}, {}, {}, {}, {}, {}, {}
+        e_f32 = keep.tile([P, PACK], F32, name="e_f32")
+
+        def quantize(name, grouped, width, pool):
+            codes = pool.tile([P, width], U32, name=name + "_codes", align_bytes=64)
+            scales = pool.tile([P, width], U8, name=name + "_scales", align_bytes=64)
+            nc.vector.quantize_mx(out=codes[:].bitcast(FP8X4), scales=scales[:], in_=grouped[:])
+            return codes, scales
+
+        def gain_fields(b, js, on_scalar):
+            if b not in planes:
+                planes[b] = work.tile([P, PACK, D], BF16, name="xe_planes", align_bytes=64)
+            for j in js:
+                src = x_sb[b, j // 2][:, j % 2, :]
+                dst = planes[b][:, j, :]
+                if b >= 2:
+                    src = src.rearrange("p (m t) -> p t m", t=PACK)
+                    dst = dst.rearrange("p (t m) -> p t m", t=PACK)
+                if on_scalar:
+                    nc.scalar.activation(out=dst, in_=src, func=ACT.Copy, scale=e_f32[:, j : j + 1])
+                else:
+                    nc.vector.tensor_scalar(out=dst, in0=src, scalar1=e_bf[:, j : j + 1], scalar2=None, op0=ALU.mult)
+
+        def interleave_xe(b, engine):
+            xe_grouped[b] = work.tile([P, D * PACK], BF16, name="xe_grouped", align_bytes=64)
+            if engine == "gpsimd":
+                dst = xe_grouped[b][:].rearrange("p (c j) -> p c j", j=PACK)
+                src = planes[b][:].rearrange("p j c -> p c j")
+                nc.gpsimd.tensor_scalar(out=dst, in0=src, scalar1=1.0, scalar2=0.0, op0=ALU.mult, op1=ALU.add)
+                return
+            dst = xe_grouped[b][:].rearrange("p (t c i j) -> p c t i j", t=PACK, i=2, j=PACK)
+            src = planes[b][:].rearrange("p j (c i t) -> p c t i j", i=2, t=PACK)
+            if engine == "vector":
+                nc.vector.tensor_copy(out=dst, in_=src)
+            else:
+                nc.scalar.copy(out=dst, in_=src)
+
+        def turn_x(b, h):
+            bank = psum.tile([P, 2, 2, P], F32, name="turn_%d" % ((2 * b + h) % TURN_BANKS))
+            turn_bank[b, h] = bank
+            for jj in range(2):
+                words = x_sb[b, h][:, jj, :].bitcast(F32)
+                for u in range(2):
+                    nc.tensor.transpose(bank[:, jj, u, :], words[:, u : 2 * P : 2], ident[:])
+
+        def empty_turn(b, h):
+            if h == 0:
+                xt_grouped[b] = work.tile([P, N * PACK], BF16, name="xt_grouped", align_bytes=64)
+            half = xt_grouped[b][:, h * 1024 : (h + 1) * 1024].bitcast(F32)
+            nc.scalar.copy(
+                out=half.rearrange("p (j r u) -> p j r u", j=2, u=2),
+                in_=turn_bank[b, h][:].rearrange("p j u r -> p j r u"),
+            )
+
+        def compress(b):
+            codes, scales = xe_q[b]
+            for h in range(HALVES):
+                bank = psum.tile([P, PACK, P], F32, name="m_%d" % h)
+                m_bank[b, h] = bank
+                ks = slice(h * P, (h + 1) * P)
+                for t in range(PACK):
+                    ds = slice(t * P, (t + 1) * P)
+                    nc.tensor.matmul_mx(
+                        out=bank[:, t, :], lhsT=codes[:, ds].bitcast(FP8X4), lhsT_scale=scales[:, ds],
+                        rhs=y_codes[:, ks].bitcast(FP8X4), rhs_scale=y_scales[:, ks], start=True, stop=True,
+                    )
+
+        def gain_dims(b):
+            mg_grouped[b] = work.tile([P, K * PACK], BF16, name="mg_grouped", align_bytes=64)
+            gains = g_bf[:].unsqueeze(1).unsqueeze(3).broadcast_to([P, P // 2, PACK, 2])
+            for h in range(HALVES):
+                dst = mg_grouped[b][:, h * 512 : (h + 1) * 512].rearrange("p (c i t) -> p c t i", i=2, t=PACK)
+                src = m_bank[b, h][:].rearrange("p t (c i) -> p c t i", i=2)
+                nc.vector.tensor_tensor(out=dst, in0=src, in1=gains, op=ALU.mult)
+
+        def interact(b):
+            codes, scales = xt_q[b]
+            mg_codes, mg_scales = mg_q[b]
+            for h in range(HALVES):
+                bank = psum.tile([P, 2, K], F32, name="f_%d" % h)
+                f_bank[b, h] = bank
+                for jj in range(2):
+                    ns = slice((2 * h + jj) * P, (2 * h + jj + 1) * P)
+                    nc.tensor.matmul_mx(
+                        out=bank[:, jj, :], lhsT=codes[:, ns].bitcast(FP8X4), lhsT_scale=scales[:, ns],
+                        rhs=mg_codes[:].bitcast(FP8X4), rhs_scale=mg_scales[:], start=True, stop=True,
+                    )
+
+        def means(b, js):
+            if b not in neg_mean:
+                neg_mean[b] = work.tile([P, PACK], F32, name="neg_mean")
+                f_scaled[b] = work.tile([P, PACK, K], F32, name="f_scaled")
+            for j in js:
+                nc.scalar.activation(
+                    out=f_scaled[b][:, j, :], in_=f_bank[b, j // 2][:, j % 2, :], func=ACT.Copy, scale=-1.0 / K,
+                    accum_out=neg_mean[b][:, j : j + 1],
+                )
+
+        def variances(b, js):
+            if b not in sq_sum:
+                sq_sum[b] = work.tile([P, PACK], F32, name="sq_sum")
+                rstd[b] = work.tile([P, PACK], F32, name="rstd")
+            for j in js:
+                squares = work.tile([P, K], BF16, name="squares")
+                nc.scalar.activation(
+                    out=squares[:], in_=f_scaled[b][:, j, :], func=ACT.Square, scale=-float(K),
+                    bias=neg_mean[b][:, j : j + 1], accum_out=sq_sum[b][:, j : j + 1],
+                )
+            cols = slice(js[0], js[-1] + 1)
+            nc.scalar.activation(
+                out=rstd[b][:, cols], in_=sq_sum[b][:, cols], func=ACT.Abs_reciprocal_sqrt, scale=1.0 / K, bias=D * EPS
+            )
+
+        def centre(b, js):
+            if b not in centred:
+                centred[b] = work.tile([P, PACK, K], F32, name="centred")
+            for j in js:
+                nc.vector.scalar_tensor_tensor(
+                    out=centred[b][:, j, :], in0=f_bank[b, j // 2][:, j % 2, :], scalar=neg_mean[b][:, j : j + 1],
+                    in1=gain_rows[:], op0=ALU.add, op1=ALU.mult,
+                )
+
+        def finish(b, js):
+            result = work.tile([P, len(js), K], F32, name="result", bufs=3, align_bytes=256)
+            for i, j in enumerate(js):
+                nc.vector.scalar_tensor_tensor(
+                    out=result[:, i, :], in0=centred[b][:, j, :], scalar=rstd[b][:, j : j + 1],
+                    in1=ln_bank[:, 1, :], op0=ALU.mult, op1=ALU.add,
+                )
+            rows = out[b].rearrange("(p j) k -> p j k", j=PACK)
+            nc.sync.dma_start(out=rows[:, js[0] : js[-1] + 1, :], in_=result[:])
+
+        y_planes = keep.tile([P, PACK, K], BF16, name="y_planes")
+        y_grouped = keep.tile([P, K * PACK], BF16, name="y_grouped", align_bytes=64)
+        for j in range(PACK):
+            nc.scalar.activation(
+                out=y_planes[:, j, :], in_=y_raw[:, j, :].bitcast(FP8), func=ACT.Copy, scale=y_row_scale[:, j : j + 1]
+            )
+        nc.scalar.copy(
+            out=y_grouped[:].rearrange("p (c i j) -> p c j i", i=4, j=PACK),
+            in_=y_planes[:].rearrange("p j (c i) -> p c j i", i=4),
+        )
+        every = list(range(PACK))
+        gain_fields(0, every, False)
+        interleave_xe(0, "vector")
+        gain_fields(1, every, False)
+        turn_x(0, 0)
+        turn_x(0, 1)
+        turn_x(1, 0)
+        empty_turn(0, 0)
+        empty_turn(0, 1)
+        y_codes, y_scales = quantize("y", y_grouped, K, keep)
+        xe_q[0] = quantize("xe", xe_grouped[0], D, work)
+        compress(0)
+        xt_q[0] = quantize("xt", xt_grouped[0], N, work)
+        interleave_xe(1, "scalar")
+        turn_x(1, 1)
+
+        ln_cols = keep.tile([P, 2, 2], F32, name="ln_cols")
+        nc.vector.tensor_copy(out=ln_cols[:, 0, :], in_=ln_g_bf[:])
+        nc.vector.tensor_copy(out=ln_cols[:, 1, :], in_=ln_b_bf[:])
+        nc.vector.tensor_copy(out=e_f32[:], in_=e_bf[:])
+        ln_bank = psum.tile([P, 2, K], F32, name="ln_bank")
+        for w in range(2):
+            for c in range(2):
+                nc.tensor.transpose(ln_bank[:, w, c : K : 2], ln_cols[:, w, c : c + 1].to_broadcast([P, P]), ident[:])
+        gain_dims(0)
+        empty_turn(1, 0)
+        empty_turn(1, 1)
+        gain_rows = keep.tile([P, K], F32, name="gain_rows")
+        nc.scalar.copy(out=gain_rows[:], in_=ln_bank[:, 0, :])
+
+        for b in range(B):
+            if b + 2 < B:
+                turn_x(b + 2, 0)
+                turn_x(b + 2, 1)
+            if b + 1 < B:
+                xe_q[b + 1] = quantize("xe", xe_grouped[b + 1], D, work)
+            if b + 2 < B:
+                gain_fields(b + 2, [0, 1], True)
+            mg_q[b] = quantize("mg", mg_grouped[b], K, work)
+            if b + 1 < B:
+                compress(b + 1)
+                xt_q[b + 1] = quantize("xt", xt_grouped[b + 1], N, work)
+            if b + 2 < B:
+                gain_fields(b + 2, [2, 3], False)
+                interleave_xe(b + 2, "gpsimd")
+                empty_turn(b + 2, 0)
+                empty_turn(b + 2, 1)
+            interact(b)
+            if b >= 1:
+                finish(b - 1, every)
+            if b + 1 < B:
+                means(b, every)
+                gain_dims(b + 1)
+                variances(b, every)
+                centre(b, every)
+            else:
+                for js in ([0, 1], [2, 3]):
+                    means(b, js)
+                    variances(b, js)
+                    centre(b, js)
+                for js in ([0, 1], [2, 3]):
+                    finish(b, js)

@@ -19,7 +19,13 @@ ALU = mybir.AluOpType
 P = 128
 PACK = 4
 HALVES = 2
-TURN_BANKS = 3
+WARM = 0
+XFIRST = 0
+YS = 0
+TAILBN = 1
+SORD = 1
+SCALAR_PLANES = [0]
+VECTOR_PLANES = [1, 2, 3]
 
 
 def tile_wukongfieldgainedlowrankfm_kernel(tc, x, e, y_bytes, y_scale, g, ln_g, ln_b, out):
@@ -44,12 +50,25 @@ def tile_wukongfieldgainedlowrankfm_kernel(tc, x, e, y_bytes, y_scale, g, ln_g, 
         ln_g_bf = keep.tile([P, 2], BF16, name="ln_g_bf")
         ln_b_bf = keep.tile([P, 2], BF16, name="ln_b_bf")
 
-        load_x(0, 0)
-        nc.sync.dma_start(out=y_raw[:], in_=y_bytes.rearrange("(p j) k -> p j k", j=PACK))
-        nc.scalar.dma_start(out=y_row_scale[:], in_=y_scale.rearrange("(p j) o -> p (j o)", j=PACK))
-        nc.scalar.dma_start(out=e_bf[:], in_=e.rearrange("(p j) -> p j", j=PACK))
-        load_x(0, 1)
-        nc.scalar.dma_start(out=g_bf[:], in_=g.rearrange("(p t) -> p t", t=PACK))
+        if XFIRST:
+            nc.scalar.dma_start(out=e_bf[:], in_=e.rearrange("(p j) -> p j", j=PACK))
+            load_x(0, 0)
+            load_x(0, 1)
+            nc.scalar.dma_start(out=y_row_scale[:], in_=y_scale.rearrange("(p j) o -> p (j o)", j=PACK))
+            nc.sync.dma_start(out=y_raw[:], in_=y_bytes.rearrange("(p j) k -> p j k", j=PACK))
+            nc.scalar.dma_start(out=g_bf[:], in_=g.rearrange("(p t) -> p t", t=PACK))
+        else:
+            nc.sync.dma_start(out=y_raw[:], in_=y_bytes.rearrange("(p j) k -> p j k", j=PACK))
+            nc.scalar.dma_start(out=y_row_scale[:], in_=y_scale.rearrange("(p j) o -> p (j o)", j=PACK))
+            load_x(0, 0)
+            nc.scalar.dma_start(out=e_bf[:], in_=e.rearrange("(p j) -> p j", j=PACK))
+            nc.scalar.dma_start(out=g_bf[:], in_=g.rearrange("(p t) -> p t", t=PACK))
+            load_x(0, 1)
+        if WARM:
+            warm_in = keep.tile([P, 1], F32, name="warm_in")
+            warm_out = keep.tile([P, 1], F32, name="warm_out")
+            nc.vector.memset(warm_in[:], 1.0)
+            nc.scalar.activation(out=warm_out[:], in_=warm_in[:], func=ACT.Abs_reciprocal_sqrt)
         load_x(1, 0)
         load_x(1, 1)
         nc.sync.dma_start(out=ln_g_bf[:], in_=ln_g.rearrange("(p c) -> p c", c=2))
@@ -63,6 +82,7 @@ def tile_wukongfieldgainedlowrankfm_kernel(tc, x, e, y_bytes, y_scale, g, ln_g, 
 
         planes, xe_grouped, xe_q, xt_grouped, xt_q, mg_grouped, mg_q = {}, {}, {}, {}, {}, {}, {}
         turn_bank, m_bank, f_bank, f_scaled, neg_mean, sq_sum, rstd, centred = {}, {}, {}, {}, {}, {}, {}, {}
+        mg_rows, mg_bank, moments, bn_tiles = {}, {}, {}, {}
         e_f32 = keep.tile([P, PACK], F32, name="e_f32")
 
         def quantize(name, grouped, width, pool):
@@ -76,14 +96,10 @@ def tile_wukongfieldgainedlowrankfm_kernel(tc, x, e, y_bytes, y_scale, g, ln_g, 
                 planes[b] = work.tile([P, PACK, D], BF16, name="xe_planes", align_bytes=64)
             for j in js:
                 src = x_sb[b, j // 2][:, j % 2, :]
-                dst = planes[b][:, j, :]
-                if b >= 2:
-                    src = src.rearrange("p (m t) -> p t m", t=PACK)
-                    dst = dst.rearrange("p (t m) -> p t m", t=PACK)
                 if on_scalar:
-                    nc.scalar.activation(out=dst, in_=src, func=ACT.Copy, scale=e_f32[:, j : j + 1])
+                    nc.scalar.activation(out=planes[b][:, j, :], in_=src, func=ACT.Copy, scale=e_f32[:, j : j + 1])
                 else:
-                    nc.vector.tensor_scalar(out=dst, in0=src, scalar1=e_bf[:, j : j + 1], scalar2=None, op0=ALU.mult)
+                    nc.vector.tensor_scalar(out=planes[b][:, j, :], in0=src, scalar1=e_bf[:, j : j + 1], scalar2=None, op0=ALU.mult)
 
         def interleave_xe(b, engine):
             xe_grouped[b] = work.tile([P, D * PACK], BF16, name="xe_grouped", align_bytes=64)
@@ -92,15 +108,15 @@ def tile_wukongfieldgainedlowrankfm_kernel(tc, x, e, y_bytes, y_scale, g, ln_g, 
                 src = planes[b][:].rearrange("p j c -> p c j")
                 nc.gpsimd.tensor_scalar(out=dst, in0=src, scalar1=1.0, scalar2=0.0, op0=ALU.mult, op1=ALU.add)
                 return
-            dst = xe_grouped[b][:].rearrange("p (t c i j) -> p c t i j", t=PACK, i=2, j=PACK)
-            src = planes[b][:].rearrange("p j (c i t) -> p c t i j", i=2, t=PACK)
+            dst = xe_grouped[b][:].rearrange("p (c i j) -> p c j i", i=4, j=PACK)
+            src = planes[b][:].rearrange("p j (c i) -> p c j i", i=4)
             if engine == "vector":
                 nc.vector.tensor_copy(out=dst, in_=src)
             else:
                 nc.scalar.copy(out=dst, in_=src)
 
         def turn_x(b, h):
-            bank = psum.tile([P, 2, 2, P], F32, name="turn_%d" % ((2 * b + h) % TURN_BANKS))
+            bank = psum.tile([P, 2, 2, P], F32, name=("f_%d" if b == 1 else "turn_%d") % h)
             turn_bank[b, h] = bank
             for jj in range(2):
                 words = x_sb[b, h][:, jj, :].bitcast(F32)
@@ -119,23 +135,36 @@ def tile_wukongfieldgainedlowrankfm_kernel(tc, x, e, y_bytes, y_scale, g, ln_g, 
         def compress(b):
             codes, scales = xe_q[b]
             for h in range(HALVES):
-                bank = psum.tile([P, PACK, P], F32, name="m_%d" % h)
-                m_bank[b, h] = bank
+                m_bank[b, h] = psum.tile([P, D], F32, name="m_%d" % h)
                 ks = slice(h * P, (h + 1) * P)
-                for t in range(PACK):
-                    ds = slice(t * P, (t + 1) * P)
-                    nc.tensor.matmul_mx(
-                        out=bank[:, t, :], lhsT=codes[:, ds].bitcast(FP8X4), lhsT_scale=scales[:, ds],
-                        rhs=y_codes[:, ks].bitcast(FP8X4), rhs_scale=y_scales[:, ks], start=True, stop=True,
-                    )
+                nc.tensor.matmul_mx(
+                    out=m_bank[b, h][:], lhsT=y_codes[:, ks].bitcast(FP8X4), lhsT_scale=y_scales[:, ks],
+                    rhs=codes[:].bitcast(FP8X4), rhs_scale=scales[:], start=True, stop=True,
+                )
 
         def gain_dims(b):
-            mg_grouped[b] = work.tile([P, K * PACK], BF16, name="mg_grouped", align_bytes=64)
-            gains = g_bf[:].unsqueeze(1).unsqueeze(3).broadcast_to([P, P // 2, PACK, 2])
             for h in range(HALVES):
-                dst = mg_grouped[b][:, h * 512 : (h + 1) * 512].rearrange("p (c i t) -> p c t i", i=2, t=PACK)
-                src = m_bank[b, h][:].rearrange("p t (c i) -> p c t i", i=2)
-                nc.vector.tensor_tensor(out=dst, in0=src, in1=gains, op=ALU.mult)
+                mg_rows[b, h] = work.tile([P, D], BF16, name="mg_rows_%d" % h, align_bytes=64)
+                nc.vector.tensor_tensor(
+                    out=mg_rows[b, h][:].rearrange("p (u q c) -> p u q c", u=2, c=2),
+                    in0=m_bank[b, h][:].rearrange("p (q u c) -> p u q c", u=2, c=2),
+                    in1=g_rows[:].rearrange("p (u q c) -> p u q c", u=2, c=2),
+                    op=ALU.mult,
+                )
+
+        def turn_mg(b):
+            mg_bank[b] = psum.tile([P, 2, 2, P], F32, name="mg_turn")
+            for h in range(HALVES):
+                words = mg_rows[b, h][:].bitcast(F32)
+                for u in range(2):
+                    nc.tensor.transpose(mg_bank[b][:, h, u, :], words[:, u * P : (u + 1) * P], ident[:])
+
+        def empty_mg_turn(b):
+            mg_grouped[b] = work.tile([P, K * PACK], BF16, name="mg_grouped", align_bytes=64)
+            nc.scalar.copy(
+                out=mg_grouped[b][:].bitcast(F32).rearrange("p (h r u) -> p h r u", h=2, u=2),
+                in_=mg_bank[b][:].rearrange("p h u r -> p h r u"),
+            )
 
         def interact(b):
             codes, scales = xt_q[b]
@@ -170,10 +199,34 @@ def tile_wukongfieldgainedlowrankfm_kernel(tc, x, e, y_bytes, y_scale, g, ln_g, 
                     out=squares[:], in_=f_scaled[b][:, j, :], func=ACT.Square, scale=-float(K),
                     bias=neg_mean[b][:, j : j + 1], accum_out=sq_sum[b][:, j : j + 1],
                 )
+
+        def inverse_std(b, js):
             cols = slice(js[0], js[-1] + 1)
             nc.scalar.activation(
                 out=rstd[b][:, cols], in_=sq_sum[b][:, cols], func=ACT.Abs_reciprocal_sqrt, scale=1.0 / K, bias=D * EPS
             )
+
+        def vector_stats(b, js):
+            stats = work.tile([P, len(js), 6], F32, name="bn_stats")
+            moments[b] = work.tile([P, len(js), 2], F32, name="moments")
+            for i, j in enumerate(js):
+                nc.vector.bn_stats(out=stats[:, i, :], in_=f_bank[b, j // 2][:, j % 2, :])
+            bn_tiles[b] = stats
+
+        def vector_moments(b, js):
+            stats = bn_tiles[b]
+            for i, j in enumerate(js):
+                nc.vector.bn_aggr(out=moments[b][:, i, :], in_=stats[:, i, :])
+            nc.scalar.activation(
+                out=rstd[b][:, js[0] : js[-1] + 1], in_=moments[b][:, :, 1], func=ACT.Abs_reciprocal_sqrt, bias=D * EPS
+            )
+
+        def centre_by_moments(b, js):
+            for i, j in enumerate(js):
+                nc.vector.scalar_tensor_tensor(
+                    out=centred[b][:, j, :], in0=f_bank[b, j // 2][:, j % 2, :], scalar=moments[b][:, i, 0:1],
+                    in1=gain_rows[:], op0=ALU.subtract, op1=ALU.mult,
+                )
 
         def centre(b, js):
             if b not in centred:
@@ -185,7 +238,7 @@ def tile_wukongfieldgainedlowrankfm_kernel(tc, x, e, y_bytes, y_scale, g, ln_g, 
                 )
 
         def finish(b, js):
-            result = work.tile([P, len(js), K], F32, name="result", bufs=3, align_bytes=256)
+            result = work.tile([P, len(js), K], F32, name="result", bufs=4, align_bytes=256)
             for i, j in enumerate(js):
                 nc.vector.scalar_tensor_tensor(
                     out=result[:, i, :], in0=centred[b][:, j, :], scalar=rstd[b][:, j : j + 1],
@@ -196,73 +249,130 @@ def tile_wukongfieldgainedlowrankfm_kernel(tc, x, e, y_bytes, y_scale, g, ln_g, 
 
         y_planes = keep.tile([P, PACK, K], BF16, name="y_planes")
         y_grouped = keep.tile([P, K * PACK], BF16, name="y_grouped", align_bytes=64)
-        for j in range(PACK):
-            nc.scalar.activation(
-                out=y_planes[:, j, :], in_=y_raw[:, j, :].bitcast(FP8), func=ACT.Copy, scale=y_row_scale[:, j : j + 1]
-            )
-        nc.scalar.copy(
-            out=y_grouped[:].rearrange("p (c i j) -> p c j i", i=4, j=PACK),
-            in_=y_planes[:].rearrange("p j (c i) -> p c j i", i=4),
-        )
         every = list(range(PACK))
+
+        def widen_y():
+            for j in range(PACK):
+                if YS:
+                    nc.scalar.activation(out=y_planes[:, j, :], in_=y_raw[:, j, :].bitcast(FP8), func=ACT.Copy, scale=y_row_scale[:, j : j + 1])
+                else:
+                    nc.vector.tensor_scalar(
+                        out=y_planes[:, j, :], in0=y_raw[:, j, :].bitcast(FP8), scalar1=y_row_scale[:, j : j + 1], scalar2=None,
+                        op0=ALU.mult,
+                    )
+            nc.scalar.copy(
+                out=y_grouped[:].rearrange("p (c i j) -> p c j i", i=4, j=PACK),
+                in_=y_planes[:].rearrange("p j (c i) -> p c j i", i=4),
+            )
+
+        if not XFIRST:
+            widen_y()
         gain_fields(0, every, False)
+        if XFIRST:
+            widen_y()
+        g_cols = keep.tile([P, PACK], F32, name="g_cols")
+        nc.vector.tensor_copy(out=g_cols[:], in_=g_bf[:])
         interleave_xe(0, "vector")
         gain_fields(1, every, False)
-        turn_x(0, 0)
-        turn_x(0, 1)
+        for h in range(HALVES):
+            turn_x(0, h)
+            empty_turn(0, h)
+        g_bank = psum.tile([P, PACK, P], F32, name="mg_turn")
+        for t in range(PACK):
+            nc.tensor.transpose(g_bank[:, t, :], g_cols[:, t : t + 1].to_broadcast([P, P]), ident[:])
+        g_rows = keep.tile([P, D], F32, name="g_rows")
+        nc.scalar.copy(
+            out=g_rows[:].rearrange("p (u q c) -> p u q c", u=2, c=2),
+            in_=g_bank[:].rearrange("p (u c) q -> p u q c", u=2),
+        )
         turn_x(1, 0)
-        empty_turn(0, 0)
-        empty_turn(0, 1)
         y_codes, y_scales = quantize("y", y_grouped, K, keep)
         xe_q[0] = quantize("xe", xe_grouped[0], D, work)
         compress(0)
+        turn_x(1, 1)
         xt_q[0] = quantize("xt", xt_grouped[0], N, work)
         interleave_xe(1, "scalar")
-        turn_x(1, 1)
-
         ln_cols = keep.tile([P, 2, 2], F32, name="ln_cols")
         nc.vector.tensor_copy(out=ln_cols[:, 0, :], in_=ln_g_bf[:])
         nc.vector.tensor_copy(out=ln_cols[:, 1, :], in_=ln_b_bf[:])
         nc.vector.tensor_copy(out=e_f32[:], in_=e_bf[:])
+        gain_dims(0)
+        turn_mg(0)
         ln_bank = psum.tile([P, 2, K], F32, name="ln_bank")
         for w in range(2):
             for c in range(2):
                 nc.tensor.transpose(ln_bank[:, w, c : K : 2], ln_cols[:, w, c : c + 1].to_broadcast([P, P]), ident[:])
-        gain_dims(0)
         empty_turn(1, 0)
         empty_turn(1, 1)
+        empty_mg_turn(0)
+        gain_fields(2, SCALAR_PLANES, True)
         gain_rows = keep.tile([P, K], F32, name="gain_rows")
         nc.scalar.copy(out=gain_rows[:], in_=ln_bank[:, 0, :])
 
         for b in range(B):
+            if b + 1 < B:
+                xe_q[b + 1] = quantize("xe", xe_grouped[b + 1], D, work)
+                compress(b + 1)
+            if b == 0:
+                xt_q[b + 1] = quantize("xt", xt_grouped[b + 1], N, work)
+            mg_q[b] = quantize("mg", mg_grouped[b], K, work)
+            interact(b)
+            if 0 < b < B - 1:
+                xt_q[b + 1] = quantize("xt", xt_grouped[b + 1], N, work)
             if b + 2 < B:
+                gain_fields(b + 2, VECTOR_PLANES, False)
+                interleave_xe(b + 2, "gpsimd")
                 turn_x(b + 2, 0)
                 turn_x(b + 2, 1)
             if b + 1 < B:
-                xe_q[b + 1] = quantize("xe", xe_grouped[b + 1], D, work)
-            if b + 2 < B:
-                gain_fields(b + 2, [0, 1], True)
-            mg_q[b] = quantize("mg", mg_grouped[b], K, work)
-            if b + 1 < B:
-                compress(b + 1)
-                xt_q[b + 1] = quantize("xt", xt_grouped[b + 1], N, work)
-            if b + 2 < B:
-                gain_fields(b + 2, [2, 3], False)
-                interleave_xe(b + 2, "gpsimd")
-                empty_turn(b + 2, 0)
-                empty_turn(b + 2, 1)
-            interact(b)
+                gain_dims(b + 1)
+                turn_mg(b + 1)
             if b >= 1:
                 finish(b - 1, every)
             if b + 1 < B:
                 means(b, every)
-                gain_dims(b + 1)
-                variances(b, every)
-                centre(b, every)
+                if b + 2 < B:
+                    if SORD == 1:
+                        empty_turn(b + 2, 0)
+                        empty_mg_turn(b + 1)
+                        empty_turn(b + 2, 1)
+                    elif SORD == 2:
+                        empty_turn(b + 2, 0)
+                        empty_turn(b + 2, 1)
+                        empty_mg_turn(b + 1)
+                    else:
+                        empty_mg_turn(b + 1)
+                        empty_turn(b + 2, 0)
+                        empty_turn(b + 2, 1)
+                    centre(b, every)
+                    if b + 3 < B:
+                        gain_fields(b + 3, SCALAR_PLANES, True)
+                    variances(b, every)
+                    inverse_std(b, every)
+                else:
+                    empty_mg_turn(b + 1)
+                    centre(b, every)
+                    variances(b, [0, 1])
+                    variances(b, [2])
+                    inverse_std(b, [0, 1])
+                    variances(b, [3])
+                    inverse_std(b, [2, 3])
+            elif TAILBN:
+                means(b, [0, 1])
+                variances(b, [0, 1])
+                vector_stats(b, [2, 3])
+                inverse_std(b, [0, 1])
+                centre(b, [0, 1])
+                vector_moments(b, [2, 3])
+                finish(b, [0, 1])
+                centre_by_moments(b, [2, 3])
+                for js in ([2], [3]):
+                    finish(b, js)
             else:
                 for js in ([0, 1], [2, 3]):
                     means(b, js)
                     variances(b, js)
+                    inverse_std(b, js)
                     centre(b, js)
-                for js in ([0, 1], [2, 3]):
+                for js in ([0, 1], [2], [3]):
                     finish(b, js)

@@ -19,7 +19,7 @@ ALU = mybir.AluOpType
 P = 128
 PACK = 4
 HALVES = 2
-WARM = 0
+WARM = 1
 XFIRST = 0
 YS = 0
 TAILBN = 1

@@ -18,18 +18,19 @@ ALU = mybir.AluOpType
 
 P = 128
 PACK = 4
+PAIR = 2
 HALVES = 2
-WARM = 1
-XFIRST = 0
-YS = 0
-TAILBN = 1
-SORD = 1
-SCALAR_PLANES = [0]
-VECTOR_PLANES = [1, 2, 3]
+RUN = 4
+ROW_GROUPS = list(range(PACK))
+SCALAR_GROUPS = [0]
+VECTOR_GROUPS = [1, 2, 3]
+SCALAR_COLUMNS = 128
+RESULT_BUFS = 6
 
 
 def tile_wukongfieldgainedlowrankfm_kernel(tc, x, e, y_bytes, y_scale, g, ln_g, ln_b, out):
     nc = tc.nc
+    last = B - 1
     with ExitStack() as ctx:
         keep = ctx.enter_context(tc.tile_pool(name="keep", bufs=1))
         work = ctx.enter_context(tc.tile_pool(name="work", bufs=2))
@@ -50,25 +51,18 @@ def tile_wukongfieldgainedlowrankfm_kernel(tc, x, e, y_bytes, y_scale, g, ln_g, 
         ln_g_bf = keep.tile([P, 2], BF16, name="ln_g_bf")
         ln_b_bf = keep.tile([P, 2], BF16, name="ln_b_bf")
 
-        if XFIRST:
-            nc.scalar.dma_start(out=e_bf[:], in_=e.rearrange("(p j) -> p j", j=PACK))
-            load_x(0, 0)
-            load_x(0, 1)
-            nc.scalar.dma_start(out=y_row_scale[:], in_=y_scale.rearrange("(p j) o -> p (j o)", j=PACK))
-            nc.sync.dma_start(out=y_raw[:], in_=y_bytes.rearrange("(p j) k -> p j k", j=PACK))
-            nc.scalar.dma_start(out=g_bf[:], in_=g.rearrange("(p t) -> p t", t=PACK))
-        else:
-            nc.sync.dma_start(out=y_raw[:], in_=y_bytes.rearrange("(p j) k -> p j k", j=PACK))
-            nc.scalar.dma_start(out=y_row_scale[:], in_=y_scale.rearrange("(p j) o -> p (j o)", j=PACK))
-            load_x(0, 0)
-            nc.scalar.dma_start(out=e_bf[:], in_=e.rearrange("(p j) -> p j", j=PACK))
-            nc.scalar.dma_start(out=g_bf[:], in_=g.rearrange("(p t) -> p t", t=PACK))
-            load_x(0, 1)
-        if WARM:
-            warm_in = keep.tile([P, 1], F32, name="warm_in")
-            warm_out = keep.tile([P, 1], F32, name="warm_out")
-            nc.vector.memset(warm_in[:], 1.0)
-            nc.scalar.activation(out=warm_out[:], in_=warm_in[:], func=ACT.Abs_reciprocal_sqrt)
+        nc.sync.dma_start(out=y_raw[:], in_=y_bytes.rearrange("(p j) k -> p j k", j=PACK))
+        nc.scalar.dma_start(out=y_row_scale[:], in_=y_scale.rearrange("(p j) o -> p (j o)", j=PACK))
+        load_x(0, 0)
+        nc.scalar.dma_start(out=e_bf[:], in_=e.rearrange("(p j) -> p j", j=PACK))
+        nc.scalar.dma_start(out=g_bf[:], in_=g.rearrange("(p t) -> p t", t=PACK))
+        load_x(0, 1)
+
+        warm_in = keep.tile([P, 1], F32, name="warm_in")
+        warm_out = keep.tile([P, 1], F32, name="warm_out")
+        nc.vector.memset(warm_in[:], 1.0)
+        nc.scalar.activation(out=warm_out[:], in_=warm_in[:], func=ACT.Abs_reciprocal_sqrt)
+
         load_x(1, 0)
         load_x(1, 1)
         nc.sync.dma_start(out=ln_g_bf[:], in_=ln_g.rearrange("(p c) -> p c", c=2))
@@ -79,57 +73,62 @@ def tile_wukongfieldgainedlowrankfm_kernel(tc, x, e, y_bytes, y_scale, g, ln_g, 
 
         ident = keep.tile([P, P], F32, name="ident")
         make_identity(nc, ident[:])
-
-        planes, xe_grouped, xe_q, xt_grouped, xt_q, mg_grouped, mg_q = {}, {}, {}, {}, {}, {}, {}
-        turn_bank, m_bank, f_bank, f_scaled, neg_mean, sq_sum, rstd, centred = {}, {}, {}, {}, {}, {}, {}, {}
-        mg_rows, mg_bank, moments, bn_tiles = {}, {}, {}, {}
         e_f32 = keep.tile([P, PACK], F32, name="e_f32")
 
-        def quantize(name, grouped, width, pool):
-            codes = pool.tile([P, width], U32, name=name + "_codes", align_bytes=64)
-            scales = pool.tile([P, width], U8, name=name + "_scales", align_bytes=64)
+        xe_rows, xe_grouped, xe_q, x_bank, xt_grouped, xt_q = {}, {}, {}, {}, {}, {}
+        m_bank, mg_rows, mg_bank, mg_grouped, mg_q = {}, {}, {}, {}, {}
+        f_rows, f_scaled, neg_mean, sq_sum, rstd, centred = {}, {}, {}, {}, {}, {}
+
+        def quantize(name, grouped, columns, pool):
+            codes = pool.tile([P, columns], U32, name=name + "_codes", align_bytes=64)
+            scales = pool.tile([P, columns], U8, name=name + "_scales", align_bytes=64)
             nc.vector.quantize_mx(out=codes[:].bitcast(FP8X4), scales=scales[:], in_=grouped[:])
             return codes, scales
 
-        def gain_fields(b, js, on_scalar):
-            if b not in planes:
-                planes[b] = work.tile([P, PACK, D], BF16, name="xe_planes", align_bytes=64)
-            for j in js:
+        def gain_fields(b, groups, engine):
+            if b not in xe_rows:
+                xe_rows[b] = work.tile([P, PACK, D], BF16, name="xe_rows", align_bytes=64)
+            for j in groups:
                 src = x_sb[b, j // 2][:, j % 2, :]
-                if on_scalar:
-                    nc.scalar.activation(out=planes[b][:, j, :], in_=src, func=ACT.Copy, scale=e_f32[:, j : j + 1])
+                dst = xe_rows[b][:, j, :]
+                if engine == "scalar":
+                    nc.scalar.activation(out=dst, in_=src, func=ACT.Copy, scale=e_f32[:, j : j + 1])
                 else:
-                    nc.vector.tensor_scalar(out=planes[b][:, j, :], in0=src, scalar1=e_bf[:, j : j + 1], scalar2=None, op0=ALU.mult)
+                    nc.vector.tensor_scalar(out=dst, in0=src, scalar1=e_bf[:, j : j + 1], scalar2=None, op0=ALU.mult)
 
-        def interleave_xe(b, engine):
-            xe_grouped[b] = work.tile([P, D * PACK], BF16, name="xe_grouped", align_bytes=64)
+        def interleave_xe(b, engine, lo=0, hi=D):
+            if b not in xe_grouped:
+                xe_grouped[b] = work.tile([P, D * PACK], BF16, name="xe_grouped", align_bytes=64)
+            grouped = xe_grouped[b][:, lo * PACK : hi * PACK]
+            columns = xe_rows[b][:, :, lo:hi]
             if engine == "gpsimd":
-                dst = xe_grouped[b][:].rearrange("p (c j) -> p c j", j=PACK)
-                src = planes[b][:].rearrange("p j c -> p c j")
-                nc.gpsimd.tensor_scalar(out=dst, in0=src, scalar1=1.0, scalar2=0.0, op0=ALU.mult, op1=ALU.add)
+                nc.gpsimd.tensor_scalar(
+                    out=grouped.rearrange("p (c j) -> p c j", j=PACK), in0=columns.rearrange("p j c -> p c j"),
+                    scalar1=1.0, scalar2=0.0, op0=ALU.mult, op1=ALU.add,
+                )
                 return
-            dst = xe_grouped[b][:].rearrange("p (c i j) -> p c j i", i=4, j=PACK)
-            src = planes[b][:].rearrange("p j (c i) -> p c j i", i=4)
+            dst = grouped.rearrange("p (c i j) -> p c j i", i=RUN, j=PACK)
+            src = columns.rearrange("p j (c i) -> p c j i", i=RUN)
             if engine == "vector":
                 nc.vector.tensor_copy(out=dst, in_=src)
             else:
                 nc.scalar.copy(out=dst, in_=src)
 
         def turn_x(b, h):
-            bank = psum.tile([P, 2, 2, P], F32, name=("f_%d" if b == 1 else "turn_%d") % h)
-            turn_bank[b, h] = bank
+            x_bank[b, h] = psum.tile([P, 2, PAIR, P], F32, name=("f_%d" if b == 1 else "turn_%d") % h)
             for jj in range(2):
                 words = x_sb[b, h][:, jj, :].bitcast(F32)
-                for u in range(2):
-                    nc.tensor.transpose(bank[:, jj, u, :], words[:, u : 2 * P : 2], ident[:])
+                for u in range(PAIR):
+                    nc.tensor.transpose(x_bank[b, h][:, jj, u, :], words[:, u : 2 * P : 2], ident[:])
 
-        def empty_turn(b, h):
+        def empty_x_bank(b, h):
             if h == 0:
                 xt_grouped[b] = work.tile([P, N * PACK], BF16, name="xt_grouped", align_bytes=64)
-            half = xt_grouped[b][:, h * 1024 : (h + 1) * 1024].bitcast(F32)
+            width = N * PACK // HALVES
+            words = xt_grouped[b][:, h * width : (h + 1) * width].bitcast(F32)
             nc.scalar.copy(
-                out=half.rearrange("p (j r u) -> p j r u", j=2, u=2),
-                in_=turn_bank[b, h][:].rearrange("p j u r -> p j r u"),
+                out=words.rearrange("p (j r u) -> p j r u", j=2, u=PAIR),
+                in_=x_bank[b, h][:].rearrange("p j u r -> p j r u"),
             )
 
         def compress(b):
@@ -146,145 +145,116 @@ def tile_wukongfieldgainedlowrankfm_kernel(tc, x, e, y_bytes, y_scale, g, ln_g, 
             for h in range(HALVES):
                 mg_rows[b, h] = work.tile([P, D], BF16, name="mg_rows_%d" % h, align_bytes=64)
                 nc.vector.tensor_tensor(
-                    out=mg_rows[b, h][:].rearrange("p (u q c) -> p u q c", u=2, c=2),
-                    in0=m_bank[b, h][:].rearrange("p (q u c) -> p u q c", u=2, c=2),
-                    in1=g_rows[:].rearrange("p (u q c) -> p u q c", u=2, c=2),
+                    out=mg_rows[b, h][:].rearrange("p (u q c) -> p u q c", u=PAIR, c=PAIR),
+                    in0=m_bank[b, h][:].rearrange("p (q u c) -> p u q c", u=PAIR, c=PAIR),
+                    in1=g_rows[:].rearrange("p (u q c) -> p u q c", u=PAIR, c=PAIR),
                     op=ALU.mult,
                 )
 
         def turn_mg(b):
-            mg_bank[b] = psum.tile([P, 2, 2, P], F32, name="mg_turn")
+            mg_bank[b] = psum.tile([P, HALVES, PAIR, P], F32, name="mg_turn")
             for h in range(HALVES):
                 words = mg_rows[b, h][:].bitcast(F32)
-                for u in range(2):
+                for u in range(PAIR):
                     nc.tensor.transpose(mg_bank[b][:, h, u, :], words[:, u * P : (u + 1) * P], ident[:])
 
-        def empty_mg_turn(b):
+        def empty_mg_bank(b):
             mg_grouped[b] = work.tile([P, K * PACK], BF16, name="mg_grouped", align_bytes=64)
             nc.scalar.copy(
-                out=mg_grouped[b][:].bitcast(F32).rearrange("p (h r u) -> p h r u", h=2, u=2),
+                out=mg_grouped[b][:].bitcast(F32).rearrange("p (h r u) -> p h r u", h=HALVES, u=PAIR),
                 in_=mg_bank[b][:].rearrange("p h u r -> p h r u"),
             )
 
         def interact(b):
             codes, scales = xt_q[b]
             mg_codes, mg_scales = mg_q[b]
-            for h in range(HALVES):
-                bank = psum.tile([P, 2, K], F32, name="f_%d" % h)
-                f_bank[b, h] = bank
-                for jj in range(2):
-                    ns = slice((2 * h + jj) * P, (2 * h + jj + 1) * P)
-                    nc.tensor.matmul_mx(
-                        out=bank[:, jj, :], lhsT=codes[:, ns].bitcast(FP8X4), lhsT_scale=scales[:, ns],
-                        rhs=mg_codes[:].bitcast(FP8X4), rhs_scale=mg_scales[:], start=True, stop=True,
-                    )
+            for j in ROW_GROUPS:
+                if b == last:
+                    bank = psum.tile([P, 2, K], F32, name=("turn_0", "turn_1", "m_0", "m_1")[j])
+                elif j % 2 == 0:
+                    bank = psum.tile([P, 2, K], F32, name="f_%d" % (j // 2))
+                f_rows[b, j] = bank[:, j % 2, :]
+                ns = slice(j * P, (j + 1) * P)
+                nc.tensor.matmul_mx(
+                    out=f_rows[b, j], lhsT=codes[:, ns].bitcast(FP8X4), lhsT_scale=scales[:, ns],
+                    rhs=mg_codes[:].bitcast(FP8X4), rhs_scale=mg_scales[:], start=True, stop=True,
+                )
 
-        def means(b, js):
+        def means(b, groups):
             if b not in neg_mean:
                 neg_mean[b] = work.tile([P, PACK], F32, name="neg_mean")
                 f_scaled[b] = work.tile([P, PACK, K], F32, name="f_scaled")
-            for j in js:
+            for j in groups:
                 nc.scalar.activation(
-                    out=f_scaled[b][:, j, :], in_=f_bank[b, j // 2][:, j % 2, :], func=ACT.Copy, scale=-1.0 / K,
+                    out=f_scaled[b][:, j, :], in_=f_rows[b, j], func=ACT.Copy, scale=-1.0 / K,
                     accum_out=neg_mean[b][:, j : j + 1],
                 )
 
-        def variances(b, js):
+        def variances(b, groups):
             if b not in sq_sum:
                 sq_sum[b] = work.tile([P, PACK], F32, name="sq_sum")
                 rstd[b] = work.tile([P, PACK], F32, name="rstd")
-            for j in js:
+            for j in groups:
                 squares = work.tile([P, K], BF16, name="squares")
                 nc.scalar.activation(
                     out=squares[:], in_=f_scaled[b][:, j, :], func=ACT.Square, scale=-float(K),
                     bias=neg_mean[b][:, j : j + 1], accum_out=sq_sum[b][:, j : j + 1],
                 )
 
-        def inverse_std(b, js):
-            cols = slice(js[0], js[-1] + 1)
+        def inverse_std(b, groups):
+            cols = slice(groups[0], groups[-1] + 1)
             nc.scalar.activation(
                 out=rstd[b][:, cols], in_=sq_sum[b][:, cols], func=ACT.Abs_reciprocal_sqrt, scale=1.0 / K, bias=D * EPS
             )
 
-        def vector_stats(b, js):
-            stats = work.tile([P, len(js), 6], F32, name="bn_stats")
-            moments[b] = work.tile([P, len(js), 2], F32, name="moments")
-            for i, j in enumerate(js):
-                nc.vector.bn_stats(out=stats[:, i, :], in_=f_bank[b, j // 2][:, j % 2, :])
-            bn_tiles[b] = stats
-
-        def vector_moments(b, js):
-            stats = bn_tiles[b]
-            for i, j in enumerate(js):
-                nc.vector.bn_aggr(out=moments[b][:, i, :], in_=stats[:, i, :])
-            nc.scalar.activation(
-                out=rstd[b][:, js[0] : js[-1] + 1], in_=moments[b][:, :, 1], func=ACT.Abs_reciprocal_sqrt, bias=D * EPS
-            )
-
-        def centre_by_moments(b, js):
-            for i, j in enumerate(js):
-                nc.vector.scalar_tensor_tensor(
-                    out=centred[b][:, j, :], in0=f_bank[b, j // 2][:, j % 2, :], scalar=moments[b][:, i, 0:1],
-                    in1=gain_rows[:], op0=ALU.subtract, op1=ALU.mult,
-                )
-
-        def centre(b, js):
+        def centre(b, groups):
             if b not in centred:
                 centred[b] = work.tile([P, PACK, K], F32, name="centred")
-            for j in js:
+            for j in groups:
                 nc.vector.scalar_tensor_tensor(
-                    out=centred[b][:, j, :], in0=f_bank[b, j // 2][:, j % 2, :], scalar=neg_mean[b][:, j : j + 1],
-                    in1=gain_rows[:], op0=ALU.add, op1=ALU.mult,
+                    out=centred[b][:, j, :], in0=f_rows[b, j], scalar=neg_mean[b][:, j : j + 1],
+                    in1=ln_g_rows[:], op0=ALU.add, op1=ALU.mult,
                 )
 
-        def finish(b, js):
-            result = work.tile([P, len(js), K], F32, name="result", bufs=4, align_bytes=256)
-            for i, j in enumerate(js):
+        def finish(b, groups):
+            result = work.tile([P, len(groups), K], F32, name="result", bufs=RESULT_BUFS, align_bytes=256)
+            for i, j in enumerate(groups):
                 nc.vector.scalar_tensor_tensor(
                     out=result[:, i, :], in0=centred[b][:, j, :], scalar=rstd[b][:, j : j + 1],
                     in1=ln_bank[:, 1, :], op0=ALU.mult, op1=ALU.add,
                 )
             rows = out[b].rearrange("(p j) k -> p j k", j=PACK)
-            nc.sync.dma_start(out=rows[:, js[0] : js[-1] + 1, :], in_=result[:])
+            nc.sync.dma_start(out=rows[:, groups[0] : groups[-1] + 1, :], in_=result[:])
 
-        y_planes = keep.tile([P, PACK, K], BF16, name="y_planes")
+        y_rows = keep.tile([P, PACK, K], BF16, name="y_rows")
         y_grouped = keep.tile([P, K * PACK], BF16, name="y_grouped", align_bytes=64)
-        every = list(range(PACK))
-
-        def widen_y():
-            for j in range(PACK):
-                if YS:
-                    nc.scalar.activation(out=y_planes[:, j, :], in_=y_raw[:, j, :].bitcast(FP8), func=ACT.Copy, scale=y_row_scale[:, j : j + 1])
-                else:
-                    nc.vector.tensor_scalar(
-                        out=y_planes[:, j, :], in0=y_raw[:, j, :].bitcast(FP8), scalar1=y_row_scale[:, j : j + 1], scalar2=None,
-                        op0=ALU.mult,
-                    )
-            nc.scalar.copy(
-                out=y_grouped[:].rearrange("p (c i j) -> p c j i", i=4, j=PACK),
-                in_=y_planes[:].rearrange("p j (c i) -> p c j i", i=4),
+        for j in ROW_GROUPS:
+            nc.vector.tensor_scalar(
+                out=y_rows[:, j, :], in0=y_raw[:, j, :].bitcast(FP8), scalar1=y_row_scale[:, j : j + 1],
+                scalar2=None, op0=ALU.mult,
             )
-
-        if not XFIRST:
-            widen_y()
-        gain_fields(0, every, False)
-        if XFIRST:
-            widen_y()
+        nc.scalar.copy(
+            out=y_grouped[:].rearrange("p (c i j) -> p c j i", i=RUN, j=PACK),
+            in_=y_rows[:].rearrange("p j (c i) -> p c j i", i=RUN),
+        )
+        gain_fields(0, ROW_GROUPS, "vector")
         g_cols = keep.tile([P, PACK], F32, name="g_cols")
         nc.vector.tensor_copy(out=g_cols[:], in_=g_bf[:])
         interleave_xe(0, "vector")
-        gain_fields(1, every, False)
+        gain_fields(1, ROW_GROUPS, "vector")
         for h in range(HALVES):
             turn_x(0, h)
-            empty_turn(0, h)
+            empty_x_bank(0, h)
+
         g_bank = psum.tile([P, PACK, P], F32, name="mg_turn")
         for t in range(PACK):
             nc.tensor.transpose(g_bank[:, t, :], g_cols[:, t : t + 1].to_broadcast([P, P]), ident[:])
         g_rows = keep.tile([P, D], F32, name="g_rows")
         nc.scalar.copy(
-            out=g_rows[:].rearrange("p (u q c) -> p u q c", u=2, c=2),
-            in_=g_bank[:].rearrange("p (u c) q -> p u q c", u=2),
+            out=g_rows[:].rearrange("p (u q c) -> p u q c", u=PAIR, c=PAIR),
+            in_=g_bank[:].rearrange("p (u c) q -> p u q c", u=PAIR),
         )
+
         turn_x(1, 0)
         y_codes, y_scales = quantize("y", y_grouped, K, keep)
         xe_q[0] = quantize("xe", xe_grouped[0], D, work)
@@ -296,83 +266,77 @@ def tile_wukongfieldgainedlowrankfm_kernel(tc, x, e, y_bytes, y_scale, g, ln_g, 
         nc.vector.tensor_copy(out=ln_cols[:, 0, :], in_=ln_g_bf[:])
         nc.vector.tensor_copy(out=ln_cols[:, 1, :], in_=ln_b_bf[:])
         nc.vector.tensor_copy(out=e_f32[:], in_=e_bf[:])
+        gain_fields(2, VECTOR_GROUPS[:-1], "vector")
         gain_dims(0)
         turn_mg(0)
+
         ln_bank = psum.tile([P, 2, K], F32, name="ln_bank")
         for w in range(2):
             for c in range(2):
                 nc.tensor.transpose(ln_bank[:, w, c : K : 2], ln_cols[:, w, c : c + 1].to_broadcast([P, P]), ident[:])
-        empty_turn(1, 0)
-        empty_turn(1, 1)
-        empty_mg_turn(0)
-        gain_fields(2, SCALAR_PLANES, True)
-        gain_rows = keep.tile([P, K], F32, name="gain_rows")
-        nc.scalar.copy(out=gain_rows[:], in_=ln_bank[:, 0, :])
+        empty_x_bank(1, 0)
+        empty_x_bank(1, 1)
+        empty_mg_bank(0)
+        gain_fields(2, SCALAR_GROUPS, "scalar")
+        ln_g_rows = keep.tile([P, K], F32, name="ln_g_rows")
+        nc.scalar.copy(out=ln_g_rows[:], in_=ln_bank[:, 0, :])
 
-        for b in range(B):
-            if b + 1 < B:
-                xe_q[b + 1] = quantize("xe", xe_grouped[b + 1], D, work)
-                compress(b + 1)
+        for b in range(last):
+            xe_q[b + 1] = quantize("xe", xe_grouped[b + 1], D, work)
+            compress(b + 1)
             if b == 0:
-                xt_q[b + 1] = quantize("xt", xt_grouped[b + 1], N, work)
+                xt_q[1] = quantize("xt", xt_grouped[1], N, work)
+            elif b > 1:
+                xt_q[b] = quantize("xt", xt_grouped[b], N, work)
             mg_q[b] = quantize("mg", mg_grouped[b], K, work)
             interact(b)
-            if 0 < b < B - 1:
-                xt_q[b + 1] = quantize("xt", xt_grouped[b + 1], N, work)
+            if b == 0:
+                gain_fields(2, VECTOR_GROUPS[-1:], "vector")
+                interleave_xe(2, "gpsimd", 0, D - SCALAR_COLUMNS)
+                interleave_xe(2, "scalar", D - SCALAR_COLUMNS, D)
+            else:
+                if b + 2 < B:
+                    gain_fields(b + 2, VECTOR_GROUPS, "vector")
+                    interleave_xe(b + 2, "gpsimd")
+                variances(b - 1, ROW_GROUPS)
+                empty_x_bank(b + 1, 0)
+                inverse_std(b - 1, ROW_GROUPS)
+                empty_x_bank(b + 1, 1)
+            gain_dims(b + 1)
+            turn_mg(b + 1)
             if b + 2 < B:
-                gain_fields(b + 2, VECTOR_PLANES, False)
-                interleave_xe(b + 2, "gpsimd")
                 turn_x(b + 2, 0)
                 turn_x(b + 2, 1)
-            if b + 1 < B:
-                gain_dims(b + 1)
-                turn_mg(b + 1)
-            if b >= 1:
-                finish(b - 1, every)
-            if b + 1 < B:
-                means(b, every)
-                if b + 2 < B:
-                    if SORD == 1:
-                        empty_turn(b + 2, 0)
-                        empty_mg_turn(b + 1)
-                        empty_turn(b + 2, 1)
-                    elif SORD == 2:
-                        empty_turn(b + 2, 0)
-                        empty_turn(b + 2, 1)
-                        empty_mg_turn(b + 1)
-                    else:
-                        empty_mg_turn(b + 1)
-                        empty_turn(b + 2, 0)
-                        empty_turn(b + 2, 1)
-                    centre(b, every)
-                    if b + 3 < B:
-                        gain_fields(b + 3, SCALAR_PLANES, True)
-                    variances(b, every)
-                    inverse_std(b, every)
-                else:
-                    empty_mg_turn(b + 1)
-                    centre(b, every)
-                    variances(b, [0, 1])
-                    variances(b, [2])
-                    inverse_std(b, [0, 1])
-                    variances(b, [3])
-                    inverse_std(b, [2, 3])
-            elif TAILBN:
-                means(b, [0, 1])
-                variances(b, [0, 1])
-                vector_stats(b, [2, 3])
-                inverse_std(b, [0, 1])
-                centre(b, [0, 1])
-                vector_moments(b, [2, 3])
-                finish(b, [0, 1])
-                centre_by_moments(b, [2, 3])
-                for js in ([2], [3]):
-                    finish(b, js)
-            else:
-                for js in ([0, 1], [2, 3]):
-                    means(b, js)
-                    variances(b, js)
-                    inverse_std(b, js)
-                    centre(b, js)
-                for js in ([0, 1], [2], [3]):
-                    finish(b, js)
+            if b > 0:
+                finish(b - 1, ROW_GROUPS)
+            means(b, ROW_GROUPS)
+            empty_mg_bank(b + 1)
+            if b + 1 < last:
+                centre(b, ROW_GROUPS)
+            if b + 3 < B:
+                gain_fields(b + 3, SCALAR_GROUPS, "scalar")
+
+        before = last - 1
+        centre(before, [0, 1])
+        xt_q[last] = quantize("xt", xt_grouped[last], N, work)
+        mg_q[last] = quantize("mg", mg_grouped[last], K, work)
+        interact(last)
+        centre(before, [2, 3])
+        variances(before, [0, 1, 2])
+        inverse_std(before, [0, 1])
+        variances(before, [3])
+        means(last, [0])
+        inverse_std(before, [2, 3])
+        finish(before, ROW_GROUPS)
+        means(last, [1])
+        variances(last, [0, 1])
+        means(last, [2])
+        inverse_std(last, [0, 1])
+        means(last, [3])
+        variances(last, [2, 3])
+        inverse_std(last, [2, 3])
+        centre(last, [0, 1])
+        finish(last, [0, 1])
+        centre(last, [2, 3])
+        finish(last, [2])
+        finish(last, [3])

@@ -22,10 +22,17 @@ PAIR = 2
 HALVES = 2
 RUN = 4
 ROW_GROUPS = list(range(PACK))
-SCALAR_GROUPS = [0]
-VECTOR_GROUPS = [1, 2, 3]
+TWO_GROUPS_FROM = 5
 SCALAR_COLUMNS = 128
 RESULT_BUFS = 6
+
+
+def scalar_groups(b):
+    return ROW_GROUPS[: 2 if b >= TWO_GROUPS_FROM else 1]
+
+
+def vector_groups(b):
+    return ROW_GROUPS[len(scalar_groups(b)) :]
 
 
 def tile_wukongfieldgainedlowrankfm_kernel(tc, x, e, y_bytes, y_scale, g, ln_g, ln_b, out):
@@ -266,7 +273,7 @@ def tile_wukongfieldgainedlowrankfm_kernel(tc, x, e, y_bytes, y_scale, g, ln_g, 
         nc.vector.tensor_copy(out=ln_cols[:, 0, :], in_=ln_g_bf[:])
         nc.vector.tensor_copy(out=ln_cols[:, 1, :], in_=ln_b_bf[:])
         nc.vector.tensor_copy(out=e_f32[:], in_=e_bf[:])
-        gain_fields(2, VECTOR_GROUPS[:-1], "vector")
+        gain_fields(2, vector_groups(2)[:-1], "vector")
         gain_dims(0)
         turn_mg(0)
 
@@ -277,7 +284,7 @@ def tile_wukongfieldgainedlowrankfm_kernel(tc, x, e, y_bytes, y_scale, g, ln_g, 
         empty_x_bank(1, 0)
         empty_x_bank(1, 1)
         empty_mg_bank(0)
-        gain_fields(2, SCALAR_GROUPS, "scalar")
+        gain_fields(2, scalar_groups(2), "scalar")
         ln_g_rows = keep.tile([P, K], F32, name="ln_g_rows")
         nc.scalar.copy(out=ln_g_rows[:], in_=ln_bank[:, 0, :])
 
@@ -291,12 +298,12 @@ def tile_wukongfieldgainedlowrankfm_kernel(tc, x, e, y_bytes, y_scale, g, ln_g, 
             mg_q[b] = quantize("mg", mg_grouped[b], K, work)
             interact(b)
             if b == 0:
-                gain_fields(2, VECTOR_GROUPS[-1:], "vector")
+                gain_fields(2, vector_groups(2)[-1:], "vector")
                 interleave_xe(2, "gpsimd", 0, D - SCALAR_COLUMNS)
                 interleave_xe(2, "scalar", D - SCALAR_COLUMNS, D)
             else:
                 if b + 2 < B:
-                    gain_fields(b + 2, VECTOR_GROUPS, "vector")
+                    gain_fields(b + 2, vector_groups(b + 2), "vector")
                     interleave_xe(b + 2, "gpsimd")
                 variances(b - 1, ROW_GROUPS)
                 empty_x_bank(b + 1, 0)
@@ -309,19 +316,22 @@ def tile_wukongfieldgainedlowrankfm_kernel(tc, x, e, y_bytes, y_scale, g, ln_g, 
                 turn_x(b + 2, 1)
             if b > 0:
                 finish(b - 1, ROW_GROUPS)
-            means(b, ROW_GROUPS)
-            empty_mg_bank(b + 1)
             if b + 1 < last:
+                means(b, ROW_GROUPS)
+                empty_mg_bank(b + 1)
                 centre(b, ROW_GROUPS)
             if b + 3 < B:
-                gain_fields(b + 3, SCALAR_GROUPS, "scalar")
+                gain_fields(b + 3, scalar_groups(b + 3), "scalar")
 
         before = last - 1
-        centre(before, [0, 1])
+        means(before, [0, 1, 2])
+        empty_mg_bank(last)
+        means(before, [3])
         xt_q[last] = quantize("xt", xt_grouped[last], N, work)
+        centre(before, [0])
         mg_q[last] = quantize("mg", mg_grouped[last], K, work)
         interact(last)
-        centre(before, [2, 3])
+        centre(before, [1, 2, 3])
         variances(before, [0, 1, 2])
         inverse_std(before, [0, 1])
         variances(before, [3])

from contextlib import ExitStack

import concourse.mybir as mybir
from concourse.masks import make_identity

B, N, D, K = 8, 512, 512, 256
EPS = 1e-5
FLOPS = 2 * 2 * B * N * D * K

F32 = mybir.dt.float32
BF16 = mybir.dt.bfloat16
U32 = mybir.dt.uint32
U8 = mybir.dt.uint8
FP8 = mybir.dt.float8_e4m3fn
FP8X4 = mybir.dt.float8_e4m3fn_x4
ACT = mybir.ActivationFunctionType
ALU = mybir.AluOpType

P = 128
PACK = 4
PAIR = 2
HALVES = 2
RUN = 4
ROW_GROUPS = list(range(PACK))
TWO_GROUPS_FROM = 5
SCALAR_COLUMNS = 128
RESULT_BUFS = 6


def scalar_groups(b):
    return ROW_GROUPS[: 2 if b >= TWO_GROUPS_FROM else 1]


def vector_groups(b):
    return ROW_GROUPS[len(scalar_groups(b)) :]


def tile_wukongfieldgainedlowrankfm_kernel(tc, x, e, y_bytes, y_scale, g, ln_g, ln_b, out):
    nc = tc.nc
    last = B - 1
    with ExitStack() as ctx:
        keep = ctx.enter_context(tc.tile_pool(name="keep", bufs=1))
        work = ctx.enter_context(tc.tile_pool(name="work", bufs=2))
        psum = ctx.enter_context(tc.psum_pool(name="psum", bufs=1))
        ctx.enter_context(tc.manual_schedule())

        x_sb = {}

        def load_x(b, h):
            x_sb[b, h] = keep.tile([P, 2, D], BF16, name="x_%d_%d" % (b, h), align_bytes=256)
            rows = x[b].rearrange("(p j) d -> p j d", j=PACK)
            nc.sync.dma_start(out=x_sb[b, h][:], in_=rows[:, 2 * h : 2 * h + 2, :])

        y_raw = keep.tile([P, PACK, K], U8, name="y_raw", align_bytes=256)
        y_row_scale = keep.tile([P, PACK], F32, name="y_row_scale")
        e_bf = keep.tile([P, PACK], BF16, name="e_bf")
        g_bf = keep.tile([P, PACK], BF16, name="g_bf")
        ln_g_bf = keep.tile([P, 2], BF16, name="ln_g_bf")
        ln_b_bf = keep.tile([P, 2], BF16, name="ln_b_bf")

        nc.sync.dma_start(out=y_raw[:], in_=y_bytes.rearrange("(p j) k -> p j k", j=PACK))
        nc.scalar.dma_start(out=y_row_scale[:], in_=y_scale.rearrange("(p j) o -> p (j o)", j=PACK))
        load_x(0, 0)
        nc.scalar.dma_start(out=e_bf[:], in_=e.rearrange("(p j) -> p j", j=PACK))
        nc.scalar.dma_start(out=g_bf[:], in_=g.rearrange("(p t) -> p t", t=PACK))
        load_x(0, 1)

        warm_in = keep.tile([P, 1], F32, name="warm_in")
        warm_out = keep.tile([P, 1], F32, name="warm_out")
        nc.vector.memset(warm_in[:], 1.0)
        nc.scalar.activation(out=warm_out[:], in_=warm_in[:], func=ACT.Abs_reciprocal_sqrt)

        load_x(1, 0)
        load_x(1, 1)
        nc.sync.dma_start(out=ln_g_bf[:], in_=ln_g.rearrange("(p c) -> p c", c=2))
        nc.sync.dma_start(out=ln_b_bf[:], in_=ln_b.rearrange("(p c) -> p c", c=2))
        for b in range(2, B):
            for h in range(HALVES):
                load_x(b, h)

        ident = keep.tile([P, P], F32, name="ident")
        make_identity(nc, ident[:])
        e_f32 = keep.tile([P, PACK], F32, name="e_f32")

        xe_rows, xe_grouped, xe_q, x_bank, xt_grouped, xt_q = {}, {}, {}, {}, {}, {}
        m_bank, mg_rows, mg_bank, mg_grouped, mg_q = {}, {}, {}, {}, {}
        f_rows, f_scaled, neg_mean, sq_sum, rstd, centred = {}, {}, {}, {}, {}, {}

        def quantize(name, grouped, columns, pool):
            codes = pool.tile([P, columns], U32, name=name + "_codes", align_bytes=64)
            scales = pool.tile([P, columns], U8, name=name + "_scales", align_bytes=64)
            nc.vector.quantize_mx(out=codes[:].bitcast(FP8X4), scales=scales[:], in_=grouped[:])
            return codes, scales

        def gain_fields(b, groups, engine):
            if b not in xe_rows:
                xe_rows[b] = work.tile([P, PACK, D], BF16, name="xe_rows", align_bytes=64)
            for j in groups:
                src = x_sb[b, j // 2][:, j % 2, :]
                dst = xe_rows[b][:, j, :]
                if engine == "scalar":
                    nc.scalar.activation(out=dst, in_=src, func=ACT.Copy, scale=e_f32[:, j : j + 1])
                else:
                    nc.vector.tensor_scalar(out=dst, in0=src, scalar1=e_bf[:, j : j + 1], scalar2=None, op0=ALU.mult)

        def interleave_xe(b, engine, lo=0, hi=D):
            if b not in xe_grouped:
                xe_grouped[b] = work.tile([P, D * PACK], BF16, name="xe_grouped", align_bytes=64)
            grouped = xe_grouped[b][:, lo * PACK : hi * PACK]
            columns = xe_rows[b][:, :, lo:hi]
            if engine == "gpsimd":
                nc.gpsimd.tensor_scalar(
                    out=grouped.rearrange("p (c j) -> p c j", j=PACK), in0=columns.rearrange("p j c -> p c j"),
                    scalar1=1.0, scalar2=0.0, op0=ALU.mult, op1=ALU.add,
                )
                return
            dst = grouped.rearrange("p (c i j) -> p c j i", i=RUN, j=PACK)
            src = columns.rearrange("p j (c i) -> p c j i", i=RUN)
            if engine == "vector":
                nc.vector.tensor_copy(out=dst, in_=src)
            else:
                nc.scalar.copy(out=dst, in_=src)

        def turn_x(b, h):
            x_bank[b, h] = psum.tile([P, 2, PAIR, P], F32, name=("f_%d" if b == 1 else "turn_%d") % h)
            for jj in range(2):
                words = x_sb[b, h][:, jj, :].bitcast(F32)
                for u in range(PAIR):
                    nc.tensor.transpose(x_bank[b, h][:, jj, u, :], words[:, u : 2 * P : 2], ident[:])

        def empty_x_bank(b, h):
            if h == 0:
                xt_grouped[b] = work.tile([P, N * PACK], BF16, name="xt_grouped", align_bytes=64)
            width = N * PACK // HALVES
            words = xt_grouped[b][:, h * width : (h + 1) * width].bitcast(F32)
            nc.scalar.copy(
                out=words.rearrange("p (j r u) -> p j r u", j=2, u=PAIR),
                in_=x_bank[b, h][:].rearrange("p j u r -> p j r u"),
            )

        def compress(b):
            codes, scales = xe_q[b]
            for h in range(HALVES):
                m_bank[b, h] = psum.tile([P, D], F32, name="m_%d" % h)
                ks = slice(h * P, (h + 1) * P)
                nc.tensor.matmul_mx(
                    out=m_bank[b, h][:], lhsT=y_codes[:, ks].bitcast(FP8X4), lhsT_scale=y_scales[:, ks],
                    rhs=codes[:].bitcast(FP8X4), rhs_scale=scales[:], start=True, stop=True,
                )

        def gain_dims(b):
            for h in range(HALVES):
                mg_rows[b, h] = work.tile([P, D], BF16, name="mg_rows_%d" % h, align_bytes=64)
                nc.vector.tensor_tensor(
                    out=mg_rows[b, h][:].rearrange("p (u q c) -> p u q c", u=PAIR, c=PAIR),
                    in0=m_bank[b, h][:].rearrange("p (q u c) -> p u q c", u=PAIR, c=PAIR),
                    in1=g_rows[:].rearrange("p (u q c) -> p u q c", u=PAIR, c=PAIR),
                    op=ALU.mult,
                )

        def turn_mg(b):
            mg_bank[b] = psum.tile([P, HALVES, PAIR, P], F32, name="mg_turn")
            for h in range(HALVES):
                words = mg_rows[b, h][:].bitcast(F32)
                for u in range(PAIR):
                    nc.tensor.transpose(mg_bank[b][:, h, u, :], words[:, u * P : (u + 1) * P], ident[:])

        def empty_mg_bank(b):
            mg_grouped[b] = work.tile([P, K * PACK], BF16, name="mg_grouped", align_bytes=64)
            nc.scalar.copy(
                out=mg_grouped[b][:].bitcast(F32).rearrange("p (h r u) -> p h r u", h=HALVES, u=PAIR),
                in_=mg_bank[b][:].rearrange("p h u r -> p h r u"),
            )

        def interact(b):
            codes, scales = xt_q[b]
            mg_codes, mg_scales = mg_q[b]
            for j in ROW_GROUPS:
                if b == last:
                    bank = psum.tile([P, 2, K], F32, name=("turn_0", "turn_1", "m_0", "m_1")[j])
                elif j % 2 == 0:
                    bank = psum.tile([P, 2, K], F32, name="f_%d" % (j // 2))
                f_rows[b, j] = bank[:, j % 2, :]
                ns = slice(j * P, (j + 1) * P)
                nc.tensor.matmul_mx(
                    out=f_rows[b, j], lhsT=codes[:, ns].bitcast(FP8X4), lhsT_scale=scales[:, ns],
                    rhs=mg_codes[:].bitcast(FP8X4), rhs_scale=mg_scales[:], start=True, stop=True,
                )

        def means(b, groups):
            if b not in neg_mean:
                neg_mean[b] = work.tile([P, PACK], F32, name="neg_mean")
                f_scaled[b] = work.tile([P, PACK, K], F32, name="f_scaled")
            for j in groups:
                nc.scalar.activation(
                    out=f_scaled[b][:, j, :], in_=f_rows[b, j], func=ACT.Copy, scale=-1.0 / K,
                    accum_out=neg_mean[b][:, j : j + 1],
                )

        def variances(b, groups):
            if b not in sq_sum:
                sq_sum[b] = work.tile([P, PACK], F32, name="sq_sum")
                rstd[b] = work.tile([P, PACK], F32, name="rstd")
            for j in groups:
                squares = work.tile([P, K], BF16, name="squares")
                nc.scalar.activation(
                    out=squares[:], in_=f_scaled[b][:, j, :], func=ACT.Square, scale=-float(K),
                    bias=neg_mean[b][:, j : j + 1], accum_out=sq_sum[b][:, j : j + 1],
                )

        def inverse_std(b, groups):
            cols = slice(groups[0], groups[-1] + 1)
            nc.scalar.activation(
                out=rstd[b][:, cols], in_=sq_sum[b][:, cols], func=ACT.Abs_reciprocal_sqrt, scale=1.0 / K, bias=D * EPS
            )

        def centre(b, groups):
            if b not in centred:
                centred[b] = work.tile([P, PACK, K], F32, name="centred")
            for j in groups:
                nc.vector.scalar_tensor_tensor(
                    out=centred[b][:, j, :], in0=f_rows[b, j], scalar=neg_mean[b][:, j : j + 1],
                    in1=ln_g_rows[:], op0=ALU.add, op1=ALU.mult,
                )

        def finish(b, groups):
            result = work.tile([P, len(groups), K], F32, name="result", bufs=RESULT_BUFS, align_bytes=256)
            for i, j in enumerate(groups):
                nc.vector.scalar_tensor_tensor(
                    out=result[:, i, :], in0=centred[b][:, j, :], scalar=rstd[b][:, j : j + 1],
                    in1=ln_bank[:, 1, :], op0=ALU.mult, op1=ALU.add,
                )
            rows = out[b].rearrange("(p j) k -> p j k", j=PACK)
            nc.sync.dma_start(out=rows[:, groups[0] : groups[-1] + 1, :], in_=result[:])

        y_rows = keep.tile([P, PACK, K], BF16, name="y_rows")
        y_grouped = keep.tile([P, K * PACK], BF16, name="y_grouped", align_bytes=64)
        for j in ROW_GROUPS:
            nc.vector.tensor_scalar(
                out=y_rows[:, j, :], in0=y_raw[:, j, :].bitcast(FP8), scalar1=y_row_scale[:, j : j + 1],
                scalar2=None, op0=ALU.mult,
            )
        nc.scalar.copy(
            out=y_grouped[:].rearrange("p (c i j) -> p c j i", i=RUN, j=PACK),
            in_=y_rows[:].rearrange("p j (c i) -> p c j i", i=RUN),
        )
        gain_fields(0, ROW_GROUPS, "vector")
        g_cols = keep.tile([P, PACK], F32, name="g_cols")
        nc.vector.tensor_copy(out=g_cols[:], in_=g_bf[:])
        interleave_xe(0, "vector")
        gain_fields(1, ROW_GROUPS, "vector")
        for h in range(HALVES):
            turn_x(0, h)
            empty_x_bank(0, h)

        g_bank = psum.tile([P, PACK, P], F32, name="mg_turn")
        for t in range(PACK):
            nc.tensor.transpose(g_bank[:, t, :], g_cols[:, t : t + 1].to_broadcast([P, P]), ident[:])
        g_rows = keep.tile([P, D], F32, name="g_rows")
        nc.scalar.copy(
            out=g_rows[:].rearrange("p (u q c) -> p u q c", u=PAIR, c=PAIR),
            in_=g_bank[:].rearrange("p (u c) q -> p u q c", u=PAIR),
        )

        turn_x(1, 0)
        y_codes, y_scales = quantize("y", y_grouped, K, keep)
        xe_q[0] = quantize("xe", xe_grouped[0], D, work)
        compress(0)
        turn_x(1, 1)
        xt_q[0] = quantize("xt", xt_grouped[0], N, work)
        interleave_xe(1, "scalar")
        ln_cols = keep.tile([P, 2, 2], F32, name="ln_cols")
        nc.vector.tensor_copy(out=ln_cols[:, 0, :], in_=ln_g_bf[:])
        nc.vector.tensor_copy(out=ln_cols[:, 1, :], in_=ln_b_bf[:])
        nc.vector.tensor_copy(out=e_f32[:], in_=e_bf[:])
        gain_fields(2, vector_groups(2)[:-1], "vector")
        gain_dims(0)
        turn_mg(0)

        ln_bank = psum.tile([P, 2, K], F32, name="ln_bank")
        for w in range(2):
            for c in range(2):
                nc.tensor.transpose(ln_bank[:, w, c : K : 2], ln_cols[:, w, c : c + 1].to_broadcast([P, P]), ident[:])
        empty_x_bank(1, 0)
        empty_x_bank(1, 1)
        empty_mg_bank(0)
        gain_fields(2, scalar_groups(2), "scalar")
        ln_g_rows = keep.tile([P, K], F32, name="ln_g_rows")
        nc.scalar.copy(out=ln_g_rows[:], in_=ln_bank[:, 0, :])

        for b in range(last):
            xe_q[b + 1] = quantize("xe", xe_grouped[b + 1], D, work)
            compress(b + 1)
            if b == 0:
                xt_q[1] = quantize("xt", xt_grouped[1], N, work)
            elif b > 1:
                xt_q[b] = quantize("xt", xt_grouped[b], N, work)
            mg_q[b] = quantize("mg", mg_grouped[b], K, work)
            interact(b)
            if b == 0:
                gain_fields(2, vector_groups(2)[-1:], "vector")
                interleave_xe(2, "gpsimd", 0, D - SCALAR_COLUMNS)
                interleave_xe(2, "scalar", D - SCALAR_COLUMNS, D)
            else:
                if b + 2 < B:
                    gain_fields(b + 2, vector_groups(b + 2), "vector")
                    interleave_xe(b + 2, "gpsimd")
                variances(b - 1, ROW_GROUPS)
                empty_x_bank(b + 1, 0)
                inverse_std(b - 1, ROW_GROUPS)
                empty_x_bank(b + 1, 1)
            gain_dims(b + 1)
            turn_mg(b + 1)
            if b + 2 < B:
                turn_x(b + 2, 0)
                turn_x(b + 2, 1)
            if b > 0:
                finish(b - 1, ROW_GROUPS)
            if b + 1 < last:
                means(b, ROW_GROUPS)
                empty_mg_bank(b + 1)
                centre(b, ROW_GROUPS)
            if b + 3 < B:
                gain_fields(b + 3, scalar_groups(b + 3), "scalar")

        before = last - 1
        means(before, [0, 1, 2])
        empty_mg_bank(last)
        means(before, [3])
        xt_q[last] = quantize("xt", xt_grouped[last], N, work)
        centre(before, [0])
        mg_q[last] = quantize("mg", mg_grouped[last], K, work)
        interact(last)
        centre(before, [1, 2, 3])
        variances(before, [0, 1, 2])
        inverse_std(before, [0, 1])
        variances(before, [3])
        means(last, [0])
        inverse_std(before, [2, 3])
        finish(before, ROW_GROUPS)
        means(last, [1])
        variances(last, [0, 1])
        means(last, [2])
        inverse_std(last, [0, 1])
        means(last, [3])
        variances(last, [2, 3])
        inverse_std(last, [2, 3])
        centre(last, [0, 1])
        finish(last, [0, 1])
        centre(last, [2, 3])
        finish(last, [2])
        finish(last, [3])
